import numpy as np, ml_dtypes
CORES = [3,7,11,15,131,135,139,143]
N = 8
import mx_ref
BF = ml_dtypes.bfloat16
def gcols(t, e):
    v = np.concatenate([t.reshape(8, 16, -1, 4), np.zeros((8, 16, 1, 4), BF)], axis=2)
    return np.ascontiguousarray(np.stack([v[g][:, e[g]] for g in range(8)])).reshape(128, -1)
def tile(rs):
    return np.stack(rs, axis=2).reshape(128, -1).astype(BF)
def pick(q, e):
    c = np.concatenate([q[0].reshape(128, -1, 4), np.zeros((128, 1, 4), np.uint8)], axis=1); s = np.concatenate([q[1], np.ones((16, 1), np.uint8)], axis=1)
    return (np.ascontiguousarray(c[:, e].reshape(128, -1)), np.ascontiguousarray(s[:, e]))
def join(*qs):
    return (np.concatenate([q[0] for q in qs], axis=1), np.concatenate([q[1] for q in qs], axis=1))
def put(q, e, v):
    c, s = q[0].reshape(128, -1, 4).copy(), q[1].copy(); c[:, e] = v[0].reshape(128, -1, 4); s[:, e] = v[1]
    return (c.reshape(128, -1), s)
def pk(c, s):
    return (np.ascontiguousarray(c), mx_ref.live(s))
def emit(q):
    return q[0], q[1]
def packed(v, rng):
    q = [mx_ref.quantize(np.ascontiguousarray(v[r])) for r in range(N)]
    return np.stack([a for a, b in q]), np.stack([mx_ref.plane(b, rng) for a, b in q])
def values_of_codes():
    e, c = np.zeros((128, 128, 4), np.float32), np.zeros((128, 2, 4), np.uint8)
    e[np.arange(128), np.arange(128), 0] = 1
    c[:127, :, 0] = np.arange(256).reshape(2, 128).T[:127]
    return mx_ref.matmul(mx_ref.quantize(e.reshape(128, 512).astype(BF)), (c.reshape(128, 8), np.full((16, 2), 127, np.uint8))).T.reshape(-1).astype(np.float64)
CODE_VALUE, SCALE_VALUE = values_of_codes(), 2.0 ** (np.arange(256) - 127.0)
def decode(q):
    return (CODE_VALUE[q[0]].reshape(16, 8, -1, 4) * SCALE_VALUE[q[1]][:, None, :, None] + 0.0).reshape(128, -1).astype(np.float32)
def f(rng, *shape):
    return mx_ref.flush((rng.standard_normal(shape, dtype=np.float32) * np.exp2(rng.integers(-2, 3, shape[:-1] + (1,)))).astype(BF))
def wide(rng, *shape, cols=0):
    v = rng.standard_normal(shape, dtype=np.float32) * np.exp2(rng.integers(-12, 13, shape)).astype(np.float32)
    if cols: v *= np.repeat(np.exp2(rng.integers(-cols, cols + 1, shape[:-2] + (1, shape[-1] // 4))) * (rng.random(shape[:-2] + (1, shape[-1] // 4)) > 0.0625), 4, axis=-1).astype(np.float32)
    return mx_ref.flush(v.astype(BF))
C, K, R = 352, 80, 3
STEP = [3, 1, 6]
def order(p):
    return np.argsort(-(p[::16] + np.float32(0.0)), axis=1, kind="stable")
def big(v):
    v = v.astype(np.float32)
    v[np.abs(v) < np.float32(2.0 ** -16)] = 0
    return v.astype(BF)
def numbers_of(rng):
    return {"x": big(f(rng, N, 128, 4 * C)), "u": np.array(f(rng, N, 128, 512)), "v": np.array(f(rng, N, 128, 512))}
def layers(rng, still=0):
    w = big(f(rng, N, 128, 2048)).reshape(N, 8, 16, 4, 8, 16, 4)
    w[:, :, :still] = 0
    w[:, :, :, :, :, :still] = 0
    return w
def weights(rng, w):
    c, p = packed(np.ascontiguousarray(w).reshape(N, 128, 2048), rng)
    return {"wc": c, "ws": p}
def signs(rng):
    return np.stack([rng.permutation(8) % 2 * 2.0 - 1.0 for r in range(N)])
def setup_inputs(rng):
    return {**numbers_of(rng), **weights(rng, layers(rng))}
def setup_inputs_ties(rng):
    d = numbers_of(rng)
    e = rng.permutation(N)
    x = d["x"].reshape(N, 8, 16, C, 4)
    for r in range(N):
        k = np.zeros(C, int) if r == e[0] else rng.permutation(C) % 3
        a = x[r][:, :8, :3].copy()
        a[:, :, 2] = 0
        x[r][:, :8] = a[:, :, k]
    x[e[1]] = 0
    u = d["u"].reshape(N, 8, 16, 8, 16, 4)
    k = u.copy()
    u[:, :, :, :, :4] = 0
    for g in range(8): u[:, g, :8, g, :4] = k[:, g, :8, g, :4]
    return {"x": x.reshape(N, 128, 4 * C), "u": u.reshape(N, 128, 512), "v": d["v"], **weights(rng, layers(rng, 8))}
def setup_inputs_near(rng):
    d = numbers_of(rng)
    x = np.zeros((N, 8, 16, C, 4), np.float32)
    d["u"].reshape(N, 128, 8, 16, 4)[:, :, :, :4] = 0
    u = d["u"].reshape(N, 128, 128, 4)
    o, c = rng.permutation(N) % 4, signs(rng)
    upper = np.arange(C) // (C // 2)
    for r in range(N):
        i = (np.arange(C) + rng.integers(0, C, (8, 1))) % C
        if o[r] == 3: i = i % (C // 2) * 2 + upper
        s = (i + 1) // 2
        size = 1.0 if o[r] < 2 else 2.0 ** -4
        z = ((s[:, :, None] >> np.arange(8)) & 1) * np.exp2(np.arange(8) - 23.0) * size
        if o[r] < 2: x[r, :, 0, :, 0] = c[r][:, None]
        if o[r] == 1:
            for g in rng.permutation(8)[:4]: x[r, g, 0, rng.integers(C), 0] *= np.float32(2.0 ** 30)
        if o[r] == 3: x[r, :, 0, :, 0] = (8 + upper) * 2.0 ** -30
        a = rng.integers(-1, 2, (8, 3, C))
        if o[r] < 2: x[r, :, 1:4, :, 0] = a
        else:
            x[r, :, 1:4, :, 0] = (5 * a * a + a) * 2.0 ** -31
            x[r, :, 1:4, :, 1] = (a - 5 * a * a) * 2.0 ** -31
        x[r, :, 8] = z[:, :, :4]
        x[r, :, 9] = z[:, :, 4:]
        x[r, :, 10:] = rng.integers(4, 8, (8, 6, C, 4)) * 2.0 ** -20 * size
        k = 1.0 if o[r] == 0 else 2.0 ** -30
        for h in range(0, 128, 16):
            for n in range(4): u[r, h + n, h + n, :2] = k
            u[r, h + 8:h + 10, h] = k
    w = np.abs(layers(rng, 10).astype(np.float32)) * np.float32(2.0 ** -6)
    return {"x": x.reshape(N, 128, 4 * C).astype(BF), "u": u.reshape(N, 128, 512), "v": d["v"], **weights(rng, w.astype(BF))}
def setup_inputs_huge(rng):
    d = numbers_of(rng)
    c = np.stack([rng.permutation(C) % 2 * 2.0 - 1.0 for r in range(N)])
    c[rng.permutation(N) < N // 2] = -1
    x = 2.0 ** 30 * (0.75 + 0.13 * rng.random((N, 128, C, 4))) * c[:, None, :, None]
    s = np.stack([signs(rng) for i in range(4)], axis=2)
    a = 2.0 ** 30 * (1 - 0.25 * rng.random((N, 128, 8, 4, 4))) * s[:, None, :, :, None]
    d["u"].reshape(N, 128, 8, 16, 4)[:, :, :, :4] = a.astype(np.float32).astype(BF)
    w = np.zeros((N, 128, 4, 128, 4), np.float32)
    i = np.arange(128)
    for b in range(4): w[:, i, b, i, b] = -1
    return {"x": x.astype(np.float32).reshape(N, 128, 4 * C).astype(BF), "u": d["u"], "v": d["v"], **weights(rng, w.astype(BF))}
def setup_inputs_votes(rng):
    d = numbers_of(rng)
    x = d["x"].reshape(N, 8, 16, C, 4)
    x[:, :, :8] = 0
    kinds = rng.permutation(8)
    for g in range(8):
        e0, a0 = rng.permutation(C)[:K], rng.integers(0, 8, C)
        s0, q = int(rng.integers(C - K + 1)), int(rng.integers(1, C // 16))
        for r in range(N):
            e, a = rng.permutation(C)[:K], rng.integers(0, 8, C)
            if kinds[g] == 0: a[:] = r
            if kinds[g] == 1:
                e = (np.arange(K) + rng.integers(C)) % C
                a[:] = 7
            if kinds[g] == 2:
                e = rng.permutation(C // 2)[:K // 2]
                e, a = np.concatenate([e, e + C // 2]), np.tile(a[:C // 2], 2)
            if kinds[g] == 3:
                s = 16 * int(rng.integers(C // 16)) + int(rng.integers(2))
                e, a = (e0 + s) % C, np.roll(a0, s)
            if kinds[g] == 4: e = np.arange(K)
            if kinds[g] == 5: e = np.arange(C - K, C)
            if kinds[g] == 6:
                e = (s0 - 16 * q * (1 - r % 2) + np.arange(K)) % C
                if r % 2 == 0: e[1] = (s0 - 16 * q + K + 16) % C
                a[:] = 7
            p = -1.0 * rng.integers(0, 2, C)
            p[e] = 1 + 0.125 * rng.integers(0, 8, K)
            x[r, g, 0, :, 0] = p.astype(BF)
            for i in range(3): x[r, g, 1 + i, :, 0] = np.where((a >> i) & 1 == 1, 1.0, -1.0 * rng.integers(0, 2, C)).astype(BF)
    d["u"].reshape(N, 128, 8, 16, 4)[:, :, :, :4] = 0
    u = d["u"].reshape(N, 128, 128, 4)
    for h in range(0, 128, 16):
        for n in range(4): u[:, h + n, h + n, 0] = 1
    return {"x": x.reshape(N, 128, 4 * C), "u": u.reshape(N, 128, 512), "v": d["v"], **weights(rng, layers(rng, 8))}
def setup_inputs_spread(rng):
    d = setup_inputs(rng)
    d["x"] = big(wide(rng, N, 128, 4 * C, cols=6))
    return d
def check_inputs(d):
    b = []
    for k in ("x", "u", "v"):
        a = np.abs(d[k].astype(np.float32))
        if not (np.isfinite(a).all() and ((a == 0) | (a >= 2.0 ** -30) & (a <= 2.0 ** 30)).all()): b.append("a value of " + k)
    none, least, most = [emit(mx_ref.quantize(np.full((128, 16), k, np.float32).astype(BF)))[1][0, 0] for k in (0.0, 2.0 ** -30, 2.0 ** 30)]
    for r in range(N):
        if ((d["wc"][r] == 0x7F) | (d["wc"][r] == 0xFF)).any(): b.append("wc: a code that is no number")
        s = mx_ref.live(d["ws"][r])
        if ((s != none) & ((s < least) | (s > most))).any(): b.append("ws: a scale out of range")
    return b
def reference(x, u, v, wc, ws):
    qu = [mx_ref.quantize(u[r]) for r in range(N)]
    lay = [pk(wc[r], ws[r]) for r in range(N)]
    now = [x[r] for r in range(N)]
    y, ol = np.zeros((N, 128, C), np.float32), np.zeros((N, 8, C), np.float32)
    oc, osc = np.zeros((N, 128, 4 * C), np.uint8), np.zeros((N, 16, C), np.uint8)
    for t in range(R):
        came, peak, key = [], [], []
        for r in range(N):
            p = mx_ref.matmul(qu[r], mx_ref.quantize(now[r]))
            e = np.sort(order(p)[:, :K], axis=1)
            a = np.take_along_axis((p[1::16] > 0) + 2 * (p[2::16] > 0) + 4 * (p[3::16] > 0), e, axis=1)
            peak.append(e)
            key.append(a + 8 * np.roll(a, -1, axis=1))
            came.append(decode(mx_ref.quantize(gcols(now[r], e))))
        made = []
        for r in range(N):
            o = (r + STEP[t]) % N
            at = (peak[o][:, None, :] - peak[r][:, :, None]) % C // 16
            same = key[o][:, None, :] == key[r][:, :, None]
            shift = np.array([16 * np.argmax(np.bincount(at[g][same[g]], minlength=C // 16)) for g in range(8)])
            place = (np.arange(C) + shift[:, None]) % C
            m = np.sum(peak[o][:, None, :] <= place[:, :, None], axis=2) - 1
            m = np.where(m < 0, K - 1, m)
            ol[r] = np.take_along_axis(peak[o], m, axis=1)
            own = now[r].astype(np.float32)
            z = ((own + gcols(came[o].astype(BF), m).astype(np.float32)) * np.float32(0.5)).astype(BF)
            q = mx_ref.quantize(z)
            made.append(tile([mx_ref.matmul(pick(lay[r], np.arange(128 * b, 128 * b + 128)), q) * np.float32(0.03125) + own[:, b::4] for b in range(4)]))
        now = made
    for r in range(N):
        q = mx_ref.quantize(now[r])
        y[r] = mx_ref.matmul(mx_ref.quantize(v[r]), q)
        oc[r], osc[r] = emit(q)
    return {"y": y, "ol": ol, "oc": oc, "osc": osc}

@@ -1,0 +1,440 @@
+from concourse.mybir import dt, AluOpType, AxisListType, ActivationFunctionType
+
+A = AluOpType
+F = ActivationFunctionType
+C, K, ROUNDS, NR = 352, 80, 3, 8
+H = 192
+STEP = [3, 1, 6]
+BIG = 1e27
+CVT_AFTER = 3
+
+BUFFERS = {
+    "bfloat16": "xb:1408 x32:1408 xh:1408 zt:1408 ub:512 vb:512 eb:528 r16:352 kl:352 dg:80 rz:80 hm:88 sf:88 sr:88 aw:88 "
+                "ar:352 at:352 junk:5632 fl:2112 sc:1056 sg:352 gt:352 ge:352 pg:352 zz:352 lt:352 pc:432 a2:96 hr:80 td:80 te:80 "
+                "cr:160 crt:160 gj:880 dx:1408 db:384",
+    "float32": "cf:24 xr:352 ct:352 srt:64 tv:16 nc:24 ka:16 jk:64 ulf:32 q6:8 rep:96 rept:96 abn:8 pa:8 p4:8 sm:40 mm:240 vt:1536 "
+               "wt:2048 cm:64 pm:80 gl:880 vx:16 vv:32 vvt:32 sab:32 s2:32 s2t:32 bs:8 pr:96 olr:352 yb:352",
+    "float8_e4m3fn_x4": "uq:128 up:384 vq:128 eq:512 wq:512 zq:352 qx0:352 qx1:352 qx2:352 qx3:352 lq0:352 lq1:352 lq2:352",
+    "uint8": "us:128 usp:384 vs:128 es:512 wsc:512 zs:352 sx0:352 sx1:352 sx2:352 sx3:352 ls0:352 ls1:352 ls2:352",
+    "int32": "ci:80 pi:8",
+    "uint16": "cu:80 o2:8 ro:2 fo:32 msg:144 lm:144",
+}
+SCRATCH = {"ps": ("psum", [128, 4096], "float32")}
+for _d, _s in BUFFERS.items():
+    for _e in _s.split():
+        SCRATCH[_e.split(":")[0]] = ("sbuf", [128, int(_e.split(":")[1])], _d)
+
+SEMAPHORES = ["qv", "qa", "qt", "qg", "sent", "ldx", "ldy", "ldu", "ldv", "ldw", "lds", "stored",
+              "aq0", "aq1", "aq2", "al0", "al1", "al2", "am0", "am1", "am2"]
+
+
+def rank_program(g, core, T, topo):
+    rank = T.rank_of(core)
+    if rank is None:
+        return
+    ops = []
+    vec = g.vector
+    eng = {"v": vec, "a": g.scalar, "t": g.tensor, "g": g, "s": g.sync}
+
+    def V(name, a=0, b=None, step=1):
+        b = SCRATCH[name][1][1] if b is None else b
+        bits = 0
+        for c in range(a, b, step):
+            bits |= 1 << c
+        return (T[name][:, a:b:step] if step != 1 else T[name][:, a:b], name, bits)
+
+    def S(name, a, count, step):
+        return V(name, a, a + (count - 1) * step + 1, step)
+
+    def back(name, a, b):
+        return (T[name][:, b - 1:(a - 1 if a else None):-1], name, V(name, a, b)[2])
+
+    def P(bank, n=C):
+        return (T.ps[:, 512 * bank:512 * bank + n], "ps", 1 << bank)
+
+    def I(win, off):
+        return (win[0].indirect(off[0]), win[1], win[2], off)
+
+    def U8(v):
+        return v[0].bitcast(dt.uint8)
+
+    def op(q, fn, reads, writes, sem=None, count=0):
+        views = [v for v in reads if isinstance(v, tuple)]
+        rd = [v[1:3] for v in views] + [v[3][1:3] for v in views + writes if len(v) > 3]
+        ops.append({"q": q, "fn": fn, "rd": rd, "wr": [v[1:3] for v in writes], "sem": sem, "count": count})
+
+    def ap(v):
+        return v[0] if isinstance(v, tuple) else v
+
+    def ts(out, in0, s1, op0, s2=None, op1=None):
+        more = [] if op1 is None else [op1]
+        op("v", lambda: vec.tensor_scalar(out[0], in0[0], ap(s1), ap(s2), op0, *more), [in0, s1, s2], [out])
+
+    def tt(out, in0, in1, o):
+        op("v", lambda: vec.tensor_tensor(out[0], in0[0], in1[0], o), [in0, in1], [out])
+
+    def cp(out, in_):
+        op("v", lambda: vec.tensor_copy(out[0], in_[0]), [in_], [out])
+
+    def red(out, in_, o):
+        op("v", lambda: vec.tensor_reduce(out[0], in_[0], AxisListType.X, o), [in_], [out])
+
+    def scan(out, d0, d1, init, op0, op1):
+        op("v", lambda: vec.tensor_tensor_scan(out[0], d0[0], d1[0], ap(init), op0, op1), [d0, d1, init], [out])
+
+    def tr(out, in_):
+        op("v", lambda: vec.transpose(out[0], in_[0]), [in_], [out])
+
+    def ms(out, c):
+        op("v", lambda: vec.memset(out[0], c), [], [out])
+
+    def quant(q, s, in_, a, b, first=None):
+        qv, sv, iv = V(q, a, b), V(s, a, b), V(in_, 4 * a, 4 * b) if first is None else V(in_, first, first + 4 * (b - a))
+        op("v", lambda: vec.quantize_mx(qv[0], sv[0], iv[0]), [iv], [qv, sv])
+
+    def act(out, in_, func, scale=1.0, bias=None, acc=None):
+        kw = {"scale": scale}
+        if bias is not None:
+            kw["bias"] = bias[0]
+        if acc is not None:
+            kw["accum_out"] = acc[0]
+        op("a", lambda: g.scalar.activation(out[0], in_[0], func, **kw), [in_, bias], [out] + ([acc] if acc else []))
+
+    def mx(bank, w, q, s, a=0, b=C):
+        out, xq, xs = P(bank, b - a), V(q, a, b), V(s, a, b)
+        op("t", lambda: g.tensor.matmul_mx(out[0], w[0][0], w[1][0], xq[0], xs[0], True, True), [w[0], w[1], xq, xs], [out])
+
+    def side(q, s, k):
+        return V(q, 128 * k, 128 * k + 128), V(s, 128 * k, 128 * k + 128)
+
+    def iota(out, pattern, base, cm=0, small=False):
+        kw = {"allow_small_or_imprecise_dtypes": True} if small else {}
+        op("g", lambda: g.iota(out[0], pattern, base, cm, **kw), [], [out])
+
+    def gcopy(out, in_, n):
+        op("g", lambda: g.affine_select(out[0], in_[0], [[0, n]], A.is_ge, 0.0, 0, 0), [in_], [out])
+
+    def load(q, out, dst, src, sem):
+        op(q, lambda: eng[q].dma_start(dst, src), [], [out], sem, 16)
+
+    totals = {"sent": 0, "stored": 0}
+
+    def store(q, dst, src, in_):
+        totals["stored"] += 16
+        op(q, lambda: eng[q].dma_start(dst, src).then_inc(T.sem.stored, 16), [in_], [])
+
+    def send(to, dst, src, in_, sem):
+        rid, pid = topo.addr(to, core)
+        totals["sent"] += len(topo.engines(core, to))
+        op("g", lambda: g.remote_dma(dst, src, T.sem[sem], T.sem.sent, pid, rid, topo.mask(core, to)), [in_], [])
+
+    def arrive(views, sem, count):
+        op(None, None, [], views, sem, count)
+
+    load("a", V("ub"), T.ub[:, :], T.u[:, :], "ldu")
+    load("s", V("xb", 0, 4 * H), T.xb[:, 0:4 * H], T.x[:, 0:4 * H], "ldx")
+    load("a", V("xb", 4 * H, 4 * C), T.xb[:, 4 * H:4 * C], T.x[:, 4 * H:4 * C], "ldy")
+    load("s", V("wq"), U8(V("wq")), T.wc[:, :], "ldw")
+    load("s", V("wsc"), T.wsc[:, :], T.ws[:, :], "lds")
+    load("s", V("vb"), T.vb[:, :], T.v[:, :], "ldv")
+    iota(V("pi", 0, 1), [[0, 1]], 0, 1)
+    iota(V("ci", 24, 30), [[1, 6]], 0)
+    iota(V("ci", 40, 48), [[32, 8]], 0)
+    iota(V("ci", 0, 16), [[16, 2], [32, 4], [0, 2]], 0)
+    iota(V("ci", 16, 24), [[16, 8]], 0)
+    iota(V("ci", 30, 40), [[1, 5], [0, 2]], 0)
+    iota(V("ci", 48, 50), [[16, 2]], 15)
+    iota(V("ci", 50, 80), [[4, 30]], 3)
+    iota(V("hm"), [[0, 22], [4, 2], [12, 2]], 0, 0, True)
+    iota(V("r16"), [[0, 22], [1, 16]], 0, 0, True)
+    for name in ("vv", "cm", "sf"):
+        ms(V(name), 0.0)
+    ts(V("pi", 1, 2), V("pi", 0, 1), 15, A.bitwise_and)
+    ts(V("pi", 2, 3), V("pi", 0, 1), 31, A.bitwise_and)
+    ms(V("msg"), 0)
+    ms(V("srt", 24, 36), -9e29)
+    cp(V("cf", 0, 2), V("pi", 1, 3))
+    qf, rf, qm = V("cf", 0, 1), V("cf", 1, 2), V("cf", 4, 5)
+    ms(V("pg", C - 8, C), float(K))
+    ts(V("cf", 16, 22), V("ci", 24, 30), 16.0, A.mult, qf, A.add)
+    ts(V("ci", 40, 48), V("ci", 40, 48), rf, A.add)
+    ts(V("cf", 2, 3), rf, 10.5, A.is_lt, 64.0 - 1.0 / 64, A.mult)
+    ts(V("cf", 3, 4), rf, -1.0, A.mult, 31.0, A.add)
+    ts(qm, qf, 16.0, A.mult, 2.0 ** 27, A.add)
+    ts(V("cf", 8, 14), V("cf", 16, 22), 0.5, A.add)
+    ts(V("cf", 14, 16), V("cf", 16, 18), 39.0, A.add)
+    ts(V("cf", 2, 3), V("cf", 2, 3), 1.0 / 64, A.add)
+    ms(V("cf", 6, 7), 193.0 * 2.0 ** 75)
+    cp(V("cu"), V("ci"))
+    ms(V("eb"), 1.0)
+    ms(V("db"), 0.0)
+    ms(V("pr"), 0.0)
+    op("g", lambda: g.affine_select(T.eb[:, :], T.eb[:, :], [[-1, 528]], A.is_equal, 0.0, 4, 4), [V("eb")], [V("eb")])
+    quant("uq", "us", "ub", 0, 128)
+    off = V("cu", 0, 24)
+    op("v", lambda: vec.tensor_copy(T.up[:, 0:384].bitcast(dt.uint32), T.uq[:, 0:128].bitcast(dt.uint32).indirect(off[0])),
+       [V("uq"), off], [V("up")])
+    op("a", lambda: g.scalar.activation(T.usp[:, 0:384], T.us[:, 0:128].indirect(off[0]), F.Copy), [V("us"), off], [V("usp")])
+    pieces = ((0, H), (H, C))
+    for h, (a, e) in enumerate(pieces):
+        quant("qx0", "sx0", "xb", a, e)
+        mx(h, side("uq", "us", 0), "qx0", "sx0", a, e)
+
+    for t in range(ROUNDS):
+        to = T.cores[(rank - STEP[t]) % NR]
+        n_in = len(topo.engines(T.cores[(rank + STEP[t]) % NR], core))
+        qx, sx, lq, ls = ["%s%d" % (n, t) for n in ("qx", "sx", "lq", "ls")]
+
+        def M(a, b, name="msg"):
+            return V(name, 48 * t + a, 48 * t + b)
+        send(to, U8(V(lq)), U8(V(qx)), V(qx), "aq%d" % t)
+        send(to, V(ls)[0], V(sx)[0], V(sx), "aq%d" % t)
+        for bank, k in ((2, 0), (3, 1), (4, 1), (5, 2), (6, 2)):
+            mx(bank, side("up", "usp", k), qx, sx)
+        tr(V("ct", 0, H), P(0, H))
+        tr(V("ct", H, C), P(1, C - H))
+        x0, x1, x2 = S("ct", 32, 6, 48), S("ct", 64, 6, 48), S("ct", 96, 6, 48)
+        t1, t2, m1 = [V("srt", 8 * k, 8 * k + 6) for k in range(3)]
+        tt(t1, x0, x1, A.max)
+        tt(t2, x0, x1, A.min)
+        tt(m1, t1, x2, A.min)
+        tt(S("srt", 25, 6, 2), t1, x2, A.max)
+        tt(V("tv", 0, 6), t2, m1, A.max)
+        tt(S("srt", 37, 6, 2), t2, m1, A.min)
+        gcopy(V("tv", 12, 14), S("ct", 0, 2, 16), 2)
+        gcopy(V("tv", 14, 15), V("ct", 320, 321), 1)
+        gcopy(V("tv", 15, 16), V("ct", 48, 49), 1)
+
+        def count_a(c, bank, v):
+            act(V("junk", C * c, C * c + C), P(bank), F.Sign, -1.0, v, V("ka", c, c + 1))
+
+        def count_v(st):
+            for i in range(3):
+                k = 3 * st + i
+                ts(V("fl", C * k, C * k + C), P(3), V("srt", 51 + 4 * i, 52 + 4 * i) if st else V("tv", 2 * i + 1, 2 * i + 2), A.is_gt)
+            for k in range(3 * st, 3 * st + 3):
+                scan(V("sc", 176 * k, 176 * k + 176), V("fl", C * k, C * k + 176), V("fl", C * k + 176, C * k + C), 0.0, A.add, A.add)
+            ts(S("nc", 13, 3, 2) if st else S("srt", 38, 3, 4), S("sc", 528 * st + 175, 3, 176), 79.5, A.subtract, BIG, A.mult)
+
+        def sides(out, keys):
+            ts(out, keys, 193.5, A.subtract, -BIG, A.mult)
+        count_a(12, 2, V("ct", 0, 1))
+        count_v(0)
+        for i in range(3):
+            count_a(2 * i, 2, V("tv", 2 * i, 2 * i + 1))
+        count_a(13, 4, V("ct", 16, 17))
+        sides(S("srt", 36, 3, 4), S("ka", 0, 3, 2))
+        scan(V("srt", 48, 60), V("srt", 24, 36), V("srt", 36, 48), 0.0, A.min, A.max)
+        gcopy(V("nc", 0, 6), S("srt", 36, 6, 2), 6)
+        gcopy(V("nc", 6, 12), S("srt", 36, 6, 2), 6)
+        gcopy(V("tv", 6, 12), S("srt", 49, 6, 2), 6)
+        iota(V("vt"), [[0, 1536]], 0, 0, True)
+        if t == 1:
+            iota(V("xr"), [[1, 352]], 0, 0, True)
+        count_a(14, 2, V("ct", 320, 321))
+        count_a(15, 4, V("ct", 48, 49))
+        count_v(1)
+        for i in range(3):
+            count_a(6 + 2 * i, 2, V("srt", 49 + 4 * i, 50 + 4 * i))
+        sides(V("nc", 18, 22), V("ka", 12, 16))
+        sides(S("nc", 12, 3, 2), S("ka", 6, 3, 2))
+        for h in range(2):
+            act(V("jk", 16 * h, 16 * h + 11), S("nc", h, 11, 2), F.Sign, 1.0, None, V("q6", 4 + h, 5 + h))
+        tt(V("ulf", 0, 16), V("tv"), V("nc", 6, 22), A.max)
+        tt(V("ulf", 16, 32), V("tv"), V("nc", 6, 22), A.min)
+        for k, o in enumerate((A.min, A.max)):
+            for h in range(2):
+                red(V("q6", 2 * k + h, 2 * k + h + 1), S("ulf", 16 * k + h, 8, 2), o)
+        for n in range(1, 4):
+            act(S("sf", n, 22, 4), S("ct", n, 22, 16), F.Sign)
+        act(V("sr"), V("sf"), F.Relu)
+        cp(V("rep"), I(V("q6", 0, 6), V("cu", 24, 30)))
+        tr(V("rept"), V("rep"))
+        act(V("jk", 32, 64), V("rept", 64, 96), F.Identity, -2.0 ** 80, V("cf", 6, 7), V("abn", 3, 4))
+        red(V("abn", 0, 1), V("rept", 0, 32), A.min)
+        red(V("abn", 1, 2), V("rept", 32, 64), A.max)
+        scan(V("aw"), V("hm"), V("sr"), 0.0, A.mult, A.add)
+        thr = V("abn", 4, 5)
+        ts(thr, V("abn", 3, 4), V("abn", 1, 2), A.max, V("abn", 0, 1), A.min)
+        act(V("sg"), P(6), F.Sign, -1.0, thr)
+        act(V("ar"), I(V("aw"), V("cu", 50, 72)), F.Copy)
+        ts(V("gt"), P(5), thr, A.is_gt, -1.0, A.mult)
+        scan(back("pg", 0, C - 1), back("gt", 1, C), back("gt", 1, C), float(K), A.add, A.max)
+        ts(V("ge"), V("sg"), 0.5, A.is_lt)
+        if t == 0:
+            ts(V("kl"), V("r16"), qf, A.is_equal, 1024.0, A.mult)
+        scan(V("zz"), V("ge"), V("pg"), 0.0, A.add, A.min)
+        for i in (3, 4):
+            act(V("junk", C * i, C * i + 304), V("zz", 48, C), F.Sign, -1.0, V("cf", 8 + i, 9 + i), V("pa", i, i + 1))
+        tr(V("at"), V("ar"))
+        for i in range(3):
+            ts(V("fl", C * i, C * i + 288), V("zz", 16 * i, 16 * i + 288), V("cf", 8 + i, 9 + i), A.is_lt, 0.5, A.subtract)
+        for i in range(3):
+            scan(V("pc", 144 * i, 144 * i + 144), V("fl", C * i, C * i + 144), V("fl", C * i + 144, C * i + 288), 16.0 * i - 32, A.add, A.add)
+        ts(M(3, 5), V("pa", 3, 5), 0.5, A.mult, 200.0, A.add)
+        ts(M(0, 3), S("pc", 143, 3, 144), 176.0, A.add)
+        ts(M(5, 6), V("pc", 143, 144), 176.0, A.add)
+        ts(V("a2"), I(V("at"), M(0, 6)), 2.0, A.mult)
+        ts(V("p4", 0, 5), M(0, 5), 4.0, A.mult)
+        if t == 0:
+            ts(V("dg"), V("r16", 0, 80), qf, A.is_equal)
+        tt(V("hr"), I(V("at"), M(0, 5)), V("a2", 1, 81), A.add)
+        if t == 0:
+            ts(V("rz"), V("r16", 0, 80), 0.5, A.is_gt)
+        act(V("xh", 0, 704), V("xb", 0, 704), F.Copy, 0.5)
+        act(V("xh", 704, 1408), V("xb", 704, 1408), F.Copy, 0.5)
+        tt(V("td"), V("hr"), V("dg"), A.mult)
+        ts(V("mm", 0, 80), V("hr"), 2.0 ** 27, A.add, qm, A.is_equal)
+        scan(V("te"), V("rz"), V("td"), 0.0, A.mult, A.add)
+        hs = S("te", 15, 5, 16)
+        ts(V("sm", 24, 29), hs, 2.0 ** 27, A.add, 2.0 ** 27, A.subtract)
+        tt(V("sm", 32, 37), hs, V("p4", 0, 5), A.add)
+        ts(M(12, 17), hs, 0.0, A.add)
+        tt(V("sm", 0, 5), V("sm", 32, 37), V("sm", 24, 29), A.subtract)
+        cp(M(6, 11), V("sm", 0, 5))
+        send(to, M(0, 18, "lm")[0], M(0, 18)[0], M(0, 18), "al%d" % t)
+        act(V("mm", 80, 160), V("mm", 0, 80), F.Copy, 4096.0)
+        ts(V("sm", 8, 13), V("sm", 0, 5), 703.5, A.is_gt, -1408.0, A.mult)
+        win = V("vt", 128, 1536)
+        cp(I(win, M(6, 11)), V("mm", 0, 80))
+        tt(V("sm", 16, 21), V("sm", 0, 5), V("sm", 8, 13), A.add)
+        scan(V("lt"), V("kl"), V("zz"), -1000.0, A.add, A.min)
+        if t == 0:
+            for b in range(4):
+                quant("eq", "es", "eb", 128 * b, 128 * b + 128, 4 - b)
+        arrive([V(lq), V(ls)], "aq%d" % t, 2 * n_in)
+        for b in range(4):
+            mx((7, 0, 1, 2)[b], side("eq", "es", b), lq, ls)
+        for b in range(4):
+            act(V("dx", C * b, C * b + C), P((7, 0, 1, 2)[b]), F.Copy, 0.5)
+        ts(V("o2", 0, 5), V("sm", 16, 21), 704.0, A.add)
+        ts(M(24, 46), S("lt", 15, 22, 16), 15.0, A.add)
+        send(to, M(24, 46, "lm")[0], M(24, 46)[0], M(24, 46), "am%d" % t)
+        tt(V("mm", 160, 240), I(win, V("o2", 0, 5)), V("mm", 80, 160), A.add)
+        cp(I(win, V("o2", 0, 5)), V("mm", 160, 240))
+        cp(V("vt", 64, 128), V("vt", 1472, 1536))
+        arrive([M(0, 18, "lm")], "al%d" % t, n_in)
+        arrive([M(24, 46, "lm")], "am%d" % t, n_in)
+        for u in range(4):
+            if u == CVT_AFTER:
+                cp(V("cm", 0, 6), M(12, 18, "lm"))
+                act(V("cr"), I(V("cm", 0, 8), V("cu", 30, 40)), F.Copy)
+            if u:
+                act(S("wt", u - 1, 160, 4), S("wt", 1407 + u, 160, 4), F.Copy)
+            scan(S("wt", 576 + u, 368, 4), S("vt", 64 + u, 368, 4), S("vt", u, 368, 4), 0.0, A.add, A.subtract)
+        act(S("wt", 3, 160, 4), S("wt", 1411, 160, 4), F.Copy)
+        tr(V("crt"), V("cr"))
+        ts(V("pm"), I(V("crt"), V("cu", 40, 45)), 2.0 ** 27, A.add, qm, A.is_equal)
+        for j in range(11):
+            gl = V("gl", 80 * j, 80 * j + 80)
+            tt(gl, I(V("wt", 640 - 64 * j, 2048 - 64 * j), M(6, 11, "lm")), V("pm"), A.mult)
+            if j < 10:
+                act(V("gj", 80 * j, 80 * j + 80), gl, F.Copy, 1.0, None, V("vx", j, j + 1))
+            else:
+                red(V("vx", j, j + 1), gl, A.add)
+        for b in range(4):
+            act(V("db", 96 * b + 16, 96 * b + 96), I(V("dx", C * b, C * b + C), M(0, 5, "lm")), F.Copy)
+        act(S("db", 15, 4, 96), S("db", 95, 4, 96), F.Copy)
+        if t == ROUNDS - 1:
+            act(V("pr", 16, 96), I(V("xr"), M(0, 5, "lm")), F.Copy)
+            act(V("pr", 15, 16), V("pr", 95, 96), F.Copy)
+        ts(V("vv", 11, 22), V("vx", 0, 11), 2.0 ** 35, A.add, 2.0 ** 35, A.subtract)
+        tt(V("vv", 0, 11), V("vx", 0, 11), V("vv", 11, 22), A.subtract)
+        cp(V("cm", 8, 30), M(24, 46, "lm"))
+        tr(V("vvt"), V("vv"))
+        cp(V("cm", 30, 52), M(24, 46, "lm"))
+        scan(V("sab"), V("rz", 0, 32), V("vvt"), 0.0, A.mult, A.add)
+        ts(V("s2"), I(V("sab"), V("cu", 48, 50)), V("cf", 2, 3), A.mult, V("cf", 3, 4), A.add)
+        if t == 0:
+            quant("vq", "vs", "vb", 0, 128)
+        tr(V("s2t"), V("s2"))
+        red(V("bs", 0, 1), V("s2t"), A.max)
+        ts(V("bs", 1, 2), V("bs", 0, 1), 2.0 ** 29, A.add, 2.0 ** 29, A.subtract)
+        ts(V("ro"), V("cf", 14, 16), V("bs", 1, 2), A.add, V("bs", 0, 1), A.subtract)
+        cp(V("fo"), I(V("cm"), V("ro")))
+
+        def zpart(b, a, e):
+            tt(S("zt", 4 * a + b, e - a, 4), I(V("db", 96 * b, 96 * b + 96), V("fo", a // 16, e // 16)), S("xh", 4 * a + b, e - a, 4), A.add)
+
+        def layer(h):
+            quant("zq", "zs", "zt", *pieces[h])
+            for b in range(4):
+                mx(4 * h + b, side("wq", "wsc", b), "zq", "zs", *pieces[h])
+
+        def state(h, b):
+            a, e = pieces[h]
+            x32 = S("x32", 4 * a + b, e - a, 4)
+            tt(x32, P(4 * h + b, e - a), x32, A.add)
+            act(S("xb", 4 * a + b, e - a, 4), x32, F.Copy, 0.03125)
+        if t == 0:
+            act(V("x32"), V("xb"), F.Copy, 32.0)
+        zpart(0, 0, C)
+        zpart(1, 0, C)
+        if t == ROUNDS - 1:
+            act(V("olr"), I(V("pr"), V("fo", 0, 22)), F.Copy)
+            store("s", T.ol[:, :], T.olr[0:128:16, :], V("olr"))
+        zpart(2, 0, H)
+        zpart(3, 0, H)
+        zpart(2, H, C)
+        layer(0)
+        zpart(3, H, C)
+        state(0, 0)
+        layer(1)
+        for k in range(1, 8):
+            state(k // 4, k % 4)
+        nq, ns = "qx%d" % (t + 1), "sx%d" % (t + 1)
+        for h in range(2):
+            quant(nq, ns, "xb", *pieces[h])
+            mx(h, side("uq", "us", 0) if t < ROUNDS - 1 else side("vq", "vs", 0), nq, ns, *pieces[h])
+    act(V("yb", 0, H), P(0, H), F.Copy)
+    store("a", T.y[:, 0:H], T.yb[:, 0:H], V("yb", 0, H))
+    store("s", T.oc[:, :], U8(V("qx3")), V("qx3"))
+    cp(V("yb", H, C), P(1, C - H))
+    store("s", T.y[:, H:C], T.yb[:, H:C], V("yb", H, C))
+    for k in range(4):
+        store("a", T.osc[4 * k:4 * k + 4, :], T.sx3[32 * k:32 * k + 4, :], V("sx3"))
+
+    emit(T, eng, ops)
+    g.sync.wait_ge(T.sem.stored, totals["stored"])
+    g.wait_ge(T.sem.sent, totals["sent"])
+
+
+def emit(T, eng, ops):
+    hist, known, clocks, waits, marked = {}, {q: {} for q in eng}, [], [], set()
+    for i, o in enumerate(ops):
+        q, deps, need = o["q"], set(), []
+        for name, bits in o["rd"]:
+            deps.update(j for j, w, b in hist.get(name, ()) if b & bits and (w or (name == "ps" and ops[j]["q"] != q)))
+        for name, bits in o["wr"]:
+            deps.update(j for j, w, b in hist.get(name, ()) if b & bits)
+        for name, bits in o["wr"]:
+            hist[name] = [(j, w, b & ~bits) for j, w, b in hist.get(name, ()) if b & ~bits] + [(i, True, bits)]
+        for name, bits in o["rd"]:
+            hist.setdefault(name, []).append((i, False, bits))
+        kn = known.get(q, {})
+        for j in sorted(deps, reverse=True):
+            key = ops[j]["sem"] or ops[j]["q"]
+            if q is None or kn.get(key, -1) >= j:
+                continue
+            need.append(j)
+            marked.add(j)
+            kn[key] = j
+            for k2, v2 in clocks[j].items():
+                kn[k2] = max(kn.get(k2, -1), v2)
+        clocks.append(dict(kn))
+        waits.append(need)
+    count, value = {q: 0 for q in eng}, {}
+    for i, o in enumerate(ops):
+        q = o["q"]
+        value[i] = (o["sem"], o["count"])
+        if q is None:
+            continue
+        for j in waits[i]:
+            eng[q].wait_ge(T.sem[value[j][0]], value[j][1])
+        ins = o["fn"]()
+        if o["sem"]:
+            ins.then_inc(T.sem[o["sem"]], o["count"])
+        elif i in marked:
+            count[q] += 1
+            ins.then_inc(T.sem["q" + q], 1)
+            value[i] = ("q" + q, count[q])

@@ -12,8 +12,8 @@ BUFFERS = {
     "bfloat16": "xb:1408 x32:1408 xh:1408 zt:1408 ub:512 vb:512 eb:528 r16:352 kl:352 dg:80 rz:80 hm:88 sf:88 sr:88 aw:88 "
                 "ar:352 at:352 junk:5632 fl:2112 sc:1056 sg:352 gt:352 ge:352 pg:352 zz:352 lt:352 pc:432 a2:96 hr:80 td:80 te:80 "
                 "cr:160 crt:160 gj:880 dx:1408 db:384",
-    "float32": "cf:24 xr:352 ct:352 srt:64 tv:16 nc:24 ka:16 jk:64 ulf:32 q6:8 rep:96 rept:96 abn:8 pa:8 p4:8 sm:40 mm:240 vt:1536 "
-               "wt:2048 cm:64 pm:80 gl:880 vx:16 vv:32 vvt:32 sab:32 s2:32 s2t:32 bs:8 pr:96 olr:352 yb:352",
+    "float32": "cf:24 xr:352 ct:352 srt:80 tv:16 nc:24 ka:16 jk:64 ulf:32 q6:8 rep:96 rept:96 abn:8 pa:8 p4:24 sm:40 mm:240 vt:1536 "
+               "wt:2112 cm:64 pm:80 gl:880 vx:16 vv:32 vvt:32 sab:32 s2:32 s2t:32 bs:8 pr:96 olr:352 yb:352",
     "float8_e4m3fn_x4": "uq:128 up:384 vq:128 eq:512 wq:512 zq:352 qx0:352 qx1:352 qx2:352 qx3:352 lq0:352 lq1:352 lq2:352",
     "uint8": "us:128 usp:384 vs:128 es:512 wsc:512 zs:352 sx0:352 sx1:352 sx2:352 sx3:352 ls0:352 ls1:352 ls2:352",
     "int32": "ci:80 pi:8",
@@ -152,7 +152,7 @@ def rank_program(g, core, T, topo):
     ts(V("pi", 1, 2), V("pi", 0, 1), 15, A.bitwise_and)
     ts(V("pi", 2, 3), V("pi", 0, 1), 31, A.bitwise_and)
     ms(V("msg"), 0)
-    ms(V("srt", 24, 36), -9e29)
+    ms(V("srt", 24, 68), -9e29)
     cp(V("cf", 0, 2), V("pi", 1, 3))
     qf, rf, qm = V("cf", 0, 1), V("cf", 1, 2), V("cf", 4, 5)
     ms(V("pg", C - 8, C), float(K))
@@ -179,6 +179,9 @@ def rank_program(g, core, T, topo):
     for h, (a, e) in enumerate(pieces):
         quant("qx0", "sx0", "xb", a, e)
         mx(h, side("uq", "us", 0), "qx0", "sx0", a, e)
+    ts(V("kl"), V("r16"), qf, A.is_equal, 1024.0, A.mult)
+    ts(V("dg"), V("r16", 0, 80), qf, A.is_equal)
+    ts(V("rz"), V("r16", 0, 80), 0.5, A.is_gt)
 
     for t in range(ROUNDS):
         to = T.cores[(rank - STEP[t]) % NR]
@@ -189,18 +192,20 @@ def rank_program(g, core, T, topo):
             return V(name, 48 * t + a, 48 * t + b)
         send(to, U8(V(lq)), U8(V(qx)), V(qx), "aq%d" % t)
         send(to, V(ls)[0], V(sx)[0], V(sx), "aq%d" % t)
-        for bank, k in ((2, 0), (3, 1), (4, 1), (5, 2), (6, 2)):
+        iota(V("vt"), [[0, 1536]], 0, 0, True)
+        for bank, k in ((2, 0), (4, 1), (3, 1), (5, 2), (6, 2)):
             mx(bank, side("up", "usp", k), qx, sx)
         tr(V("ct", 0, H), P(0, H))
         tr(V("ct", H, C), P(1, C - H))
         x0, x1, x2 = S("ct", 32, 6, 48), S("ct", 64, 6, 48), S("ct", 96, 6, 48)
-        t1, t2, m1 = [V("srt", 8 * k, 8 * k + 6) for k in range(3)]
+        t1, t2 = S("srt", 0, 6, 2), S("srt", 1, 6, 2)
         tt(t1, x0, x1, A.max)
         tt(t2, x0, x1, A.min)
-        tt(m1, t1, x2, A.min)
-        tt(S("srt", 25, 6, 2), t1, x2, A.max)
-        tt(V("tv", 0, 6), t2, m1, A.max)
-        tt(S("srt", 37, 6, 2), t2, m1, A.min)
+        cp(S("srt", 25, 6, 2), x2)
+        tt(S("srt", 41, 6, 2), t1, x2, A.max)
+        scan(V("srt", 12, 24), V("srt", 24, 36), V("srt", 0, 12), 0.0, A.min, A.max)
+        tt(S("srt", 57, 6, 2), t2, x2, A.min)
+        gcopy(V("tv", 0, 6), S("srt", 13, 6, 2), 6)
         gcopy(V("tv", 12, 14), S("ct", 0, 2, 16), 2)
         gcopy(V("tv", 14, 15), V("ct", 320, 321), 1)
         gcopy(V("tv", 15, 16), V("ct", 48, 49), 1)
@@ -208,35 +213,40 @@ def rank_program(g, core, T, topo):
         def count_a(c, bank, v):
             act(V("junk", C * c, C * c + C), P(bank), F.Sign, -1.0, v, V("ka", c, c + 1))
 
-        def count_v(st):
-            for i in range(3):
-                k = 3 * st + i
-                ts(V("fl", C * k, C * k + C), P(3), V("srt", 51 + 4 * i, 52 + 4 * i) if st else V("tv", 2 * i + 1, 2 * i + 2), A.is_gt)
-            for k in range(3 * st, 3 * st + 3):
-                scan(V("sc", 176 * k, 176 * k + 176), V("fl", C * k, C * k + 176), V("fl", C * k + 176, C * k + C), 0.0, A.add, A.add)
-            ts(S("nc", 13, 3, 2) if st else S("srt", 38, 3, 4), S("sc", 528 * st + 175, 3, 176), 79.5, A.subtract, BIG, A.mult)
+        def flags(k, v):
+            ts(V("fl", C * k, C * k + C), P(3), v, A.is_gt, 2.0 ** 90, A.mult)
+
+        def count_v(k):
+            scan(V("sc", 176 * k, 176 * k + 176), V("fl", C * k, C * k + 176), V("fl", C * k + 176, C * k + C), -79.5 * 2.0 ** 90, A.add, A.add)
 
         def sides(out, keys):
             ts(out, keys, 193.5, A.subtract, -BIG, A.mult)
         count_a(12, 2, V("ct", 0, 1))
-        count_v(0)
-        for i in range(3):
-            count_a(2 * i, 2, V("tv", 2 * i, 2 * i + 1))
         count_a(13, 4, V("ct", 16, 17))
-        sides(S("srt", 36, 3, 4), S("ka", 0, 3, 2))
-        scan(V("srt", 48, 60), V("srt", 24, 36), V("srt", 36, 48), 0.0, A.min, A.max)
-        gcopy(V("nc", 0, 6), S("srt", 36, 6, 2), 6)
-        gcopy(V("nc", 6, 12), S("srt", 36, 6, 2), 6)
-        gcopy(V("tv", 6, 12), S("srt", 49, 6, 2), 6)
-        iota(V("vt"), [[0, 1536]], 0, 0, True)
-        if t == 1:
-            iota(V("xr"), [[1, 352]], 0, 0, True)
+        for i in range(3):
+            flags(i, V("srt", 15 + 4 * i, 16 + 4 * i))
+            count_a(2 * i, 2, V("srt", 13 + 4 * i, 14 + 4 * i))
+        for i in range(3):
+            count_v(i)
+        sides(S("srt", 56, 3, 4), S("ka", 0, 3, 2))
+        for i in range(3):
+            ts(V("tv", 7 + 2 * i, 8 + 2 * i), V("sc", 176 * i + 175, 176 * i + 176), V("srt", 43 + 4 * i, 44 + 4 * i), A.min,
+               V("srt", 59 + 4 * i, 60 + 4 * i), A.max)
+        scan(V("srt", 68, 80), V("srt", 40, 52), V("srt", 56, 68), 0.0, A.min, A.max)
+        flags(3, V("tv", 7, 8))
+        gcopy(S("tv", 6, 3, 2), S("srt", 69, 3, 4), 3)
+        gcopy(S("nc", 6, 3, 2), S("srt", 56, 3, 4), 3)
+        cp(S("nc", 7, 3, 2), S("sc", 175, 3, 176))
+        gcopy(V("nc", 0, 6), V("nc", 6, 12), 6)
         count_a(14, 2, V("ct", 320, 321))
         count_a(15, 4, V("ct", 48, 49))
-        count_v(1)
+        flags(4, V("tv", 9, 10))
+        flags(5, V("tv", 11, 12))
         for i in range(3):
-            count_a(6 + 2 * i, 2, V("srt", 49 + 4 * i, 50 + 4 * i))
+            count_a(6 + 2 * i, 2, V("srt", 69 + 4 * i, 70 + 4 * i))
+            count_v(3 + i)
         sides(V("nc", 18, 22), V("ka", 12, 16))
+        cp(S("nc", 13, 3, 2), S("sc", 703, 3, 176))
         sides(S("nc", 12, 3, 2), S("ka", 6, 3, 2))
         for h in range(2):
             act(V("jk", 16 * h, 16 * h + 11), S("nc", h, 11, 2), F.Sign, 1.0, None, V("q6", 4 + h, 5 + h))
@@ -257,12 +267,10 @@ def rank_program(g, core, T, topo):
         thr = V("abn", 4, 5)
         ts(thr, V("abn", 3, 4), V("abn", 1, 2), A.max, V("abn", 0, 1), A.min)
         act(V("sg"), P(6), F.Sign, -1.0, thr)
-        act(V("ar"), I(V("aw"), V("cu", 50, 72)), F.Copy)
         ts(V("gt"), P(5), thr, A.is_gt, -1.0, A.mult)
+        act(V("ar"), I(V("aw"), V("cu", 50, 72)), F.Copy)
         scan(back("pg", 0, C - 1), back("gt", 1, C), back("gt", 1, C), float(K), A.add, A.max)
         ts(V("ge"), V("sg"), 0.5, A.is_lt)
-        if t == 0:
-            ts(V("kl"), V("r16"), qf, A.is_equal, 1024.0, A.mult)
         scan(V("zz"), V("ge"), V("pg"), 0.0, A.add, A.min)
         for i in (3, 4):
             act(V("junk", C * i, C * i + 304), V("zz", 48, C), F.Sign, -1.0, V("cf", 8 + i, 9 + i), V("pa", i, i + 1))
@@ -276,13 +284,10 @@ def rank_program(g, core, T, topo):
         ts(M(5, 6), V("pc", 143, 144), 176.0, A.add)
         ts(V("a2"), I(V("at"), M(0, 6)), 2.0, A.mult)
         ts(V("p4", 0, 5), M(0, 5), 4.0, A.mult)
-        if t == 0:
-            ts(V("dg"), V("r16", 0, 80), qf, A.is_equal)
         tt(V("hr"), I(V("at"), M(0, 5)), V("a2", 1, 81), A.add)
-        if t == 0:
-            ts(V("rz"), V("r16", 0, 80), 0.5, A.is_gt)
         act(V("xh", 0, 704), V("xb", 0, 704), F.Copy, 0.5)
         act(V("xh", 704, 1408), V("xb", 704, 1408), F.Copy, 0.5)
+        ts(V("p4", 8, 13), M(0, 5), 175.5, A.is_gt, -1408.0, A.mult)
         tt(V("td"), V("hr"), V("dg"), A.mult)
         ts(V("mm", 0, 80), V("hr"), 2.0 ** 27, A.add, qm, A.is_equal)
         scan(V("te"), V("rz"), V("td"), 0.0, A.mult, A.add)
@@ -292,12 +297,12 @@ def rank_program(g, core, T, topo):
         ts(M(12, 17), hs, 0.0, A.add)
         tt(V("sm", 0, 5), V("sm", 32, 37), V("sm", 24, 29), A.subtract)
         cp(M(6, 11), V("sm", 0, 5))
+        tt(V("sm", 16, 21), V("sm", 0, 5), V("p4", 8, 13), A.add)
         send(to, M(0, 18, "lm")[0], M(0, 18)[0], M(0, 18), "al%d" % t)
         act(V("mm", 80, 160), V("mm", 0, 80), F.Copy, 4096.0)
-        ts(V("sm", 8, 13), V("sm", 0, 5), 703.5, A.is_gt, -1408.0, A.mult)
-        win = V("vt", 128, 1536)
+        win = V("vt", 64, 1472)
         cp(I(win, M(6, 11)), V("mm", 0, 80))
-        tt(V("sm", 16, 21), V("sm", 0, 5), V("sm", 8, 13), A.add)
+        ts(V("o2", 0, 5), V("sm", 16, 21), 704.0, A.add)
         scan(V("lt"), V("kl"), V("zz"), -1000.0, A.add, A.min)
         if t == 0:
             for b in range(4):
@@ -307,12 +312,12 @@ def rank_program(g, core, T, topo):
             mx((7, 0, 1, 2)[b], side("eq", "es", b), lq, ls)
         for b in range(4):
             act(V("dx", C * b, C * b + C), P((7, 0, 1, 2)[b]), F.Copy, 0.5)
-        ts(V("o2", 0, 5), V("sm", 16, 21), 704.0, A.add)
+        tt(V("mm", 160, 240), I(win, V("o2", 0, 5)), V("mm", 80, 160), A.add)
         ts(M(24, 46), S("lt", 15, 22, 16), 15.0, A.add)
         send(to, M(24, 46, "lm")[0], M(24, 46)[0], M(24, 46), "am%d" % t)
-        tt(V("mm", 160, 240), I(win, V("o2", 0, 5)), V("mm", 80, 160), A.add)
+        if t == 0:
+            iota(V("xr"), [[1, 352]], 0, 0, True)
         cp(I(win, V("o2", 0, 5)), V("mm", 160, 240))
-        cp(V("vt", 64, 128), V("vt", 1472, 1536))
         arrive([M(0, 18, "lm")], "al%d" % t, n_in)
         arrive([M(24, 46, "lm")], "am%d" % t, n_in)
         for u in range(4):
@@ -321,17 +326,18 @@ def rank_program(g, core, T, topo):
                 act(V("cr"), I(V("cm", 0, 8), V("cu", 30, 40)), F.Copy)
             if u:
                 act(S("wt", u - 1, 160, 4), S("wt", 1407 + u, 160, 4), F.Copy)
-            scan(S("wt", 576 + u, 368, 4), S("vt", 64 + u, 368, 4), S("vt", u, 368, 4), 0.0, A.add, A.subtract)
+            scan(S("wt", 640 + u, 368, 4), S("vt", 64 + u, 368, 4), S("vt", u, 368, 4), 0.0, A.add, A.subtract)
         act(S("wt", 3, 160, 4), S("wt", 1411, 160, 4), F.Copy)
         tr(V("crt"), V("cr"))
+        tt(V("wt", 640, 704), V("wt", 640, 704), V("wt", 2048, 2112), A.add)
         ts(V("pm"), I(V("crt"), V("cu", 40, 45)), 2.0 ** 27, A.add, qm, A.is_equal)
         for j in range(11):
             gl = V("gl", 80 * j, 80 * j + 80)
             tt(gl, I(V("wt", 640 - 64 * j, 2048 - 64 * j), M(6, 11, "lm")), V("pm"), A.mult)
-            if j < 10:
+            if j < 9:
                 act(V("gj", 80 * j, 80 * j + 80), gl, F.Copy, 1.0, None, V("vx", j, j + 1))
-            else:
-                red(V("vx", j, j + 1), gl, A.add)
+        for j in (9, 10):
+            red(V("vx", j, j + 1), V("gl", 80 * j, 80 * j + 80), A.add)
         for b in range(4):
             act(V("db", 96 * b + 16, 96 * b + 96), I(V("dx", C * b, C * b + C), M(0, 5, "lm")), F.Copy)
         act(S("db", 15, 4, 96), S("db", 95, 4, 96), F.Copy)
@@ -352,6 +358,8 @@ def rank_program(g, core, T, topo):
         ts(V("bs", 1, 2), V("bs", 0, 1), 2.0 ** 29, A.add, 2.0 ** 29, A.subtract)
         ts(V("ro"), V("cf", 14, 16), V("bs", 1, 2), A.add, V("bs", 0, 1), A.subtract)
         cp(V("fo"), I(V("cm"), V("ro")))
+        nq, ns = "qx%d" % (t + 1), "sx%d" % (t + 1)
+        nxt = side("uq", "us", 0) if t < ROUNDS - 1 else side("vq", "vs", 0)
 
         def zpart(b, a, e):
             tt(S("zt", 4 * a + b, e - a, 4), I(V("db", 96 * b, 96 * b + 96), V("fo", a // 16, e // 16)), S("xh", 4 * a + b, e - a, 4), A.add)
@@ -365,27 +373,30 @@ def rank_program(g, core, T, topo):
             a, e = pieces[h]
             x32 = S("x32", 4 * a + b, e - a, 4)
             tt(x32, P(4 * h + b, e - a), x32, A.add)
-            act(S("xb", 4 * a + b, e - a, 4), x32, F.Copy, 0.03125)
+            if (h, b) == (1, 3):
+                quant(nq, ns, "xb", 0, H)
+                mx(0, nxt, nq, ns, 0, H)
+                ts(S("xb", 4 * a + b, e - a, 4), x32, 0.03125, A.mult)
+            else:
+                act(S("xb", 4 * a + b, e - a, 4), x32, F.Copy, 0.03125)
         if t == 0:
             act(V("x32"), V("xb"), F.Copy, 32.0)
         zpart(0, 0, C)
-        zpart(1, 0, C)
         if t == ROUNDS - 1:
             act(V("olr"), I(V("pr"), V("fo", 0, 22)), F.Copy)
             store("s", T.ol[:, :], T.olr[0:128:16, :], V("olr"))
-        zpart(2, 0, H)
-        zpart(3, 0, H)
-        zpart(2, H, C)
+        for b in (1, 2, 3):
+            zpart(b, 0, H)
+        zpart(1, H, C)
         layer(0)
+        zpart(2, H, C)
         zpart(3, H, C)
         state(0, 0)
         layer(1)
         for k in range(1, 8):
             state(k // 4, k % 4)
-        nq, ns = "qx%d" % (t + 1), "sx%d" % (t + 1)
-        for h in range(2):
-            quant(nq, ns, "xb", *pieces[h])
-            mx(h, side("uq", "us", 0) if t < ROUNDS - 1 else side("vq", "vs", 0), nq, ns, *pieces[h])
+        quant(nq, ns, "xb", H, C)
+        mx(1, nxt, nq, ns, H, C)
     act(V("yb", 0, H), P(0, H), F.Copy)
     store("a", T.y[:, 0:H], T.yb[:, 0:H], V("yb", 0, H))
     store("s", T.oc[:, :], U8(V("qx3")), V("qx3"))

from concourse.mybir import dt, AluOpType, AxisListType, ActivationFunctionType

A = AluOpType
F = ActivationFunctionType
C, K, ROUNDS, NR = 352, 80, 3, 8
H = 192
STEP = [3, 1, 6]
BIG = 1e27
CVT_AFTER = 3

BUFFERS = {
    "bfloat16": "xb:1408 x32:1408 xh:1408 zt:1408 ub:512 vb:512 eb:528 r16:352 kl:352 dg:80 rz:80 hm:88 sf:88 sr:88 aw:88 "
                "ar:352 at:352 junk:5632 fl:2112 sc:1056 sg:352 gt:352 ge:352 pg:352 zz:352 lt:352 pc:432 a2:96 hr:80 td:80 te:80 "
                "cr:160 crt:160 gj:880 dx:1408 db:384",
    "float32": "cf:24 xr:352 ct:352 srt:80 tv:16 nc:24 ka:16 jk:64 ulf:32 q6:8 rep:96 rept:96 abn:8 pa:8 p4:24 sm:40 mm:240 vt:1536 "
               "wt:2112 cm:64 pm:80 gl:880 vx:16 vv:32 vvt:32 sab:32 s2:32 s2t:32 bs:8 pr:96 olr:352 yb:352",
    "float8_e4m3fn_x4": "uq:128 up:384 vq:128 eq:512 wq:512 zq:352 qx0:352 qx1:352 qx2:352 qx3:352 lq0:352 lq1:352 lq2:352",
    "uint8": "us:128 usp:384 vs:128 es:512 wsc:512 zs:352 sx0:352 sx1:352 sx2:352 sx3:352 ls0:352 ls1:352 ls2:352",
    "int32": "ci:80 pi:8",
    "uint16": "cu:80 o2:8 ro:2 fo:32 msg:144 lm:144",
}
SCRATCH = {"ps": ("psum", [128, 4096], "float32")}
for _d, _s in BUFFERS.items():
    for _e in _s.split():
        SCRATCH[_e.split(":")[0]] = ("sbuf", [128, int(_e.split(":")[1])], _d)

SEMAPHORES = ["qv", "qa", "qt", "qg", "sent", "ldx", "ldy", "ldu", "ldv", "ldw", "lds", "stored",
              "aq0", "aq1", "aq2", "al0", "al1", "al2", "am0", "am1", "am2"]


def rank_program(g, core, T, topo):
    rank = T.rank_of(core)
    if rank is None:
        return
    ops = []
    vec = g.vector
    eng = {"v": vec, "a": g.scalar, "t": g.tensor, "g": g, "s": g.sync}

    def V(name, a=0, b=None, step=1):
        b = SCRATCH[name][1][1] if b is None else b
        bits = 0
        for c in range(a, b, step):
            bits |= 1 << c
        return (T[name][:, a:b:step] if step != 1 else T[name][:, a:b], name, bits)

    def S(name, a, count, step):
        return V(name, a, a + (count - 1) * step + 1, step)

    def back(name, a, b):
        return (T[name][:, b - 1:(a - 1 if a else None):-1], name, V(name, a, b)[2])

    def P(bank, n=C):
        return (T.ps[:, 512 * bank:512 * bank + n], "ps", 1 << bank)

    def I(win, off):
        return (win[0].indirect(off[0]), win[1], win[2], off)

    def U8(v):
        return v[0].bitcast(dt.uint8)

    def op(q, fn, reads, writes, sem=None, count=0):
        views = [v for v in reads if isinstance(v, tuple)]
        rd = [v[1:3] for v in views] + [v[3][1:3] for v in views + writes if len(v) > 3]
        ops.append({"q": q, "fn": fn, "rd": rd, "wr": [v[1:3] for v in writes], "sem": sem, "count": count})

    def ap(v):
        return v[0] if isinstance(v, tuple) else v

    def ts(out, in0, s1, op0, s2=None, op1=None):
        more = [] if op1 is None else [op1]
        op("v", lambda: vec.tensor_scalar(out[0], in0[0], ap(s1), ap(s2), op0, *more), [in0, s1, s2], [out])

    def tt(out, in0, in1, o):
        op("v", lambda: vec.tensor_tensor(out[0], in0[0], in1[0], o), [in0, in1], [out])

    def cp(out, in_):
        op("v", lambda: vec.tensor_copy(out[0], in_[0]), [in_], [out])

    def red(out, in_, o):
        op("v", lambda: vec.tensor_reduce(out[0], in_[0], AxisListType.X, o), [in_], [out])

    def scan(out, d0, d1, init, op0, op1):
        op("v", lambda: vec.tensor_tensor_scan(out[0], d0[0], d1[0], ap(init), op0, op1), [d0, d1, init], [out])

    def tr(out, in_):
        op("v", lambda: vec.transpose(out[0], in_[0]), [in_], [out])

    def ms(out, c):
        op("v", lambda: vec.memset(out[0], c), [], [out])

    def quant(q, s, in_, a, b, first=None):
        qv, sv, iv = V(q, a, b), V(s, a, b), V(in_, 4 * a, 4 * b) if first is None else V(in_, first, first + 4 * (b - a))
        op("v", lambda: vec.quantize_mx(qv[0], sv[0], iv[0]), [iv], [qv, sv])

    def act(out, in_, func, scale=1.0, bias=None, acc=None):
        kw = {"scale": scale}
        if bias is not None:
            kw["bias"] = bias[0]
        if acc is not None:
            kw["accum_out"] = acc[0]
        op("a", lambda: g.scalar.activation(out[0], in_[0], func, **kw), [in_, bias], [out] + ([acc] if acc else []))

    def mx(bank, w, q, s, a=0, b=C):
        out, xq, xs = P(bank, b - a), V(q, a, b), V(s, a, b)
        op("t", lambda: g.tensor.matmul_mx(out[0], w[0][0], w[1][0], xq[0], xs[0], True, True), [w[0], w[1], xq, xs], [out])

    def side(q, s, k):
        return V(q, 128 * k, 128 * k + 128), V(s, 128 * k, 128 * k + 128)

    def iota(out, pattern, base, cm=0, small=False):
        kw = {"allow_small_or_imprecise_dtypes": True} if small else {}
        op("g", lambda: g.iota(out[0], pattern, base, cm, **kw), [], [out])

    def gcopy(out, in_, n):
        op("g", lambda: g.affine_select(out[0], in_[0], [[0, n]], A.is_ge, 0.0, 0, 0), [in_], [out])

    def load(q, out, dst, src, sem):
        op(q, lambda: eng[q].dma_start(dst, src), [], [out], sem, 16)

    totals = {"sent": 0, "stored": 0}

    def store(q, dst, src, in_):
        totals["stored"] += 16
        op(q, lambda: eng[q].dma_start(dst, src).then_inc(T.sem.stored, 16), [in_], [])

    def send(to, dst, src, in_, sem):
        rid, pid = topo.addr(to, core)
        totals["sent"] += len(topo.engines(core, to))
        op("g", lambda: g.remote_dma(dst, src, T.sem[sem], T.sem.sent, pid, rid, topo.mask(core, to)), [in_], [])

    def arrive(views, sem, count):
        op(None, None, [], views, sem, count)

    load("a", V("ub"), T.ub[:, :], T.u[:, :], "ldu")
    load("s", V("xb", 0, 4 * H), T.xb[:, 0:4 * H], T.x[:, 0:4 * H], "ldx")
    load("a", V("xb", 4 * H, 4 * C), T.xb[:, 4 * H:4 * C], T.x[:, 4 * H:4 * C], "ldy")
    load("s", V("wq"), U8(V("wq")), T.wc[:, :], "ldw")
    load("s", V("wsc"), T.wsc[:, :], T.ws[:, :], "lds")
    load("s", V("vb"), T.vb[:, :], T.v[:, :], "ldv")
    iota(V("pi", 0, 1), [[0, 1]], 0, 1)
    iota(V("ci", 24, 30), [[1, 6]], 0)
    iota(V("ci", 40, 48), [[32, 8]], 0)
    iota(V("ci", 0, 16), [[16, 2], [32, 4], [0, 2]], 0)
    iota(V("ci", 16, 24), [[16, 8]], 0)
    iota(V("ci", 30, 40), [[1, 5], [0, 2]], 0)
    iota(V("ci", 48, 50), [[16, 2]], 15)
    iota(V("ci", 50, 80), [[4, 30]], 3)
    iota(V("hm"), [[0, 22], [4, 2], [12, 2]], 0, 0, True)
    iota(V("r16"), [[0, 22], [1, 16]], 0, 0, True)
    for name in ("vv", "cm", "sf"):
        ms(V(name), 0.0)
    ts(V("pi", 1, 2), V("pi", 0, 1), 15, A.bitwise_and)
    ts(V("pi", 2, 3), V("pi", 0, 1), 31, A.bitwise_and)
    ms(V("msg"), 0)
    ms(V("srt", 24, 68), -9e29)
    cp(V("cf", 0, 2), V("pi", 1, 3))
    qf, rf, qm = V("cf", 0, 1), V("cf", 1, 2), V("cf", 4, 5)
    ms(V("pg", C - 8, C), float(K))
    ts(V("cf", 16, 22), V("ci", 24, 30), 16.0, A.mult, qf, A.add)
    ts(V("ci", 40, 48), V("ci", 40, 48), rf, A.add)
    ts(V("cf", 2, 3), rf, 10.5, A.is_lt, 64.0 - 1.0 / 64, A.mult)
    ts(V("cf", 3, 4), rf, -1.0, A.mult, 31.0, A.add)
    ts(qm, qf, 16.0, A.mult, 2.0 ** 27, A.add)
    ts(V("cf", 8, 14), V("cf", 16, 22), 0.5, A.add)
    ts(V("cf", 14, 16), V("cf", 16, 18), 39.0, A.add)
    ts(V("cf", 2, 3), V("cf", 2, 3), 1.0 / 64, A.add)
    ms(V("cf", 6, 7), 193.0 * 2.0 ** 75)
    cp(V("cu"), V("ci"))
    ms(V("eb"), 1.0)
    ms(V("db"), 0.0)
    ms(V("pr"), 0.0)
    op("g", lambda: g.affine_select(T.eb[:, :], T.eb[:, :], [[-1, 528]], A.is_equal, 0.0, 4, 4), [V("eb")], [V("eb")])
    quant("uq", "us", "ub", 0, 128)
    off = V("cu", 0, 24)
    op("v", lambda: vec.tensor_copy(T.up[:, 0:384].bitcast(dt.uint32), T.uq[:, 0:128].bitcast(dt.uint32).indirect(off[0])),
       [V("uq"), off], [V("up")])
    op("a", lambda: g.scalar.activation(T.usp[:, 0:384], T.us[:, 0:128].indirect(off[0]), F.Copy), [V("us"), off], [V("usp")])
    pieces = ((0, H), (H, C))
    for h, (a, e) in enumerate(pieces):
        quant("qx0", "sx0", "xb", a, e)
        mx(h, side("uq", "us", 0), "qx0", "sx0", a, e)
    ts(V("kl"), V("r16"), qf, A.is_equal, 1024.0, A.mult)
    ts(V("dg"), V("r16", 0, 80), qf, A.is_equal)
    ts(V("rz"), V("r16", 0, 80), 0.5, A.is_gt)

    for t in range(ROUNDS):
        to = T.cores[(rank - STEP[t]) % NR]
        n_in = len(topo.engines(T.cores[(rank + STEP[t]) % NR], core))
        qx, sx, lq, ls = ["%s%d" % (n, t) for n in ("qx", "sx", "lq", "ls")]

        def M(a, b, name="msg"):
            return V(name, 48 * t + a, 48 * t + b)
        send(to, U8(V(lq)), U8(V(qx)), V(qx), "aq%d" % t)
        send(to, V(ls)[0], V(sx)[0], V(sx), "aq%d" % t)
        iota(V("vt"), [[0, 1536]], 0, 0, True)
        for bank, k in ((2, 0), (4, 1), (3, 1), (5, 2), (6, 2)):
            mx(bank, side("up", "usp", k), qx, sx)
        tr(V("ct", 0, H), P(0, H))
        tr(V("ct", H, C), P(1, C - H))
        x0, x1, x2 = S("ct", 32, 6, 48), S("ct", 64, 6, 48), S("ct", 96, 6, 48)
        t1, t2 = S("srt", 0, 6, 2), S("srt", 1, 6, 2)
        tt(t1, x0, x1, A.max)
        tt(t2, x0, x1, A.min)
        cp(S("srt", 25, 6, 2), x2)
        tt(S("srt", 41, 6, 2), t1, x2, A.max)
        scan(V("srt", 12, 24), V("srt", 24, 36), V("srt", 0, 12), 0.0, A.min, A.max)
        tt(S("srt", 57, 6, 2), t2, x2, A.min)
        gcopy(V("tv", 0, 6), S("srt", 13, 6, 2), 6)
        gcopy(V("tv", 12, 14), S("ct", 0, 2, 16), 2)
        gcopy(V("tv", 14, 15), V("ct", 320, 321), 1)
        gcopy(V("tv", 15, 16), V("ct", 48, 49), 1)

        def count_a(c, bank, v):
            act(V("junk", C * c, C * c + C), P(bank), F.Sign, -1.0, v, V("ka", c, c + 1))

        def flags(k, v):
            ts(V("fl", C * k, C * k + C), P(3), v, A.is_gt, 2.0 ** 90, A.mult)

        def count_v(k):
            scan(V("sc", 176 * k, 176 * k + 176), V("fl", C * k, C * k + 176), V("fl", C * k + 176, C * k + C), -79.5 * 2.0 ** 90, A.add, A.add)

        def sides(out, keys):
            ts(out, keys, 193.5, A.subtract, -BIG, A.mult)
        count_a(12, 2, V("ct", 0, 1))
        count_a(13, 4, V("ct", 16, 17))
        for i in range(3):
            flags(i, V("srt", 15 + 4 * i, 16 + 4 * i))
            count_a(2 * i, 2, V("srt", 13 + 4 * i, 14 + 4 * i))
        for i in range(3):
            count_v(i)
        sides(S("srt", 56, 3, 4), S("ka", 0, 3, 2))
        for i in range(3):
            ts(V("tv", 7 + 2 * i, 8 + 2 * i), V("sc", 176 * i + 175, 176 * i + 176), V("srt", 43 + 4 * i, 44 + 4 * i), A.min,
               V("srt", 59 + 4 * i, 60 + 4 * i), A.max)
        scan(V("srt", 68, 80), V("srt", 40, 52), V("srt", 56, 68), 0.0, A.min, A.max)
        flags(3, V("tv", 7, 8))
        gcopy(S("tv", 6, 3, 2), S("srt", 69, 3, 4), 3)
        gcopy(S("nc", 6, 3, 2), S("srt", 56, 3, 4), 3)
        cp(S("nc", 7, 3, 2), S("sc", 175, 3, 176))
        gcopy(V("nc", 0, 6), V("nc", 6, 12), 6)
        count_a(14, 2, V("ct", 320, 321))
        count_a(15, 4, V("ct", 48, 49))
        flags(4, V("tv", 9, 10))
        flags(5, V("tv", 11, 12))
        for i in range(3):
            count_a(6 + 2 * i, 2, V("srt", 69 + 4 * i, 70 + 4 * i))
            count_v(3 + i)
        sides(V("nc", 18, 22), V("ka", 12, 16))
        cp(S("nc", 13, 3, 2), S("sc", 703, 3, 176))
        sides(S("nc", 12, 3, 2), S("ka", 6, 3, 2))
        for h in range(2):
            act(V("jk", 16 * h, 16 * h + 11), S("nc", h, 11, 2), F.Sign, 1.0, None, V("q6", 4 + h, 5 + h))
        tt(V("ulf", 0, 16), V("tv"), V("nc", 6, 22), A.max)
        tt(V("ulf", 16, 32), V("tv"), V("nc", 6, 22), A.min)
        for k, o in enumerate((A.min, A.max)):
            for h in range(2):
                red(V("q6", 2 * k + h, 2 * k + h + 1), S("ulf", 16 * k + h, 8, 2), o)
        for n in range(1, 4):
            act(S("sf", n, 22, 4), S("ct", n, 22, 16), F.Sign)
        act(V("sr"), V("sf"), F.Relu)
        cp(V("rep"), I(V("q6", 0, 6), V("cu", 24, 30)))
        tr(V("rept"), V("rep"))
        act(V("jk", 32, 64), V("rept", 64, 96), F.Identity, -2.0 ** 80, V("cf", 6, 7), V("abn", 3, 4))
        red(V("abn", 0, 1), V("rept", 0, 32), A.min)
        red(V("abn", 1, 2), V("rept", 32, 64), A.max)
        scan(V("aw"), V("hm"), V("sr"), 0.0, A.mult, A.add)
        thr = V("abn", 4, 5)
        ts(thr, V("abn", 3, 4), V("abn", 1, 2), A.max, V("abn", 0, 1), A.min)
        act(V("sg"), P(6), F.Sign, -1.0, thr)
        ts(V("gt"), P(5), thr, A.is_gt, -1.0, A.mult)
        act(V("ar"), I(V("aw"), V("cu", 50, 72)), F.Copy)
        scan(back("pg", 0, C - 1), back("gt", 1, C), back("gt", 1, C), float(K), A.add, A.max)
        ts(V("ge"), V("sg"), 0.5, A.is_lt)
        scan(V("zz"), V("ge"), V("pg"), 0.0, A.add, A.min)
        for i in (3, 4):
            act(V("junk", C * i, C * i + 304), V("zz", 48, C), F.Sign, -1.0, V("cf", 8 + i, 9 + i), V("pa", i, i + 1))
        tr(V("at"), V("ar"))
        for i in range(3):
            ts(V("fl", C * i, C * i + 288), V("zz", 16 * i, 16 * i + 288), V("cf", 8 + i, 9 + i), A.is_lt, 0.5, A.subtract)
        for i in range(3):
            scan(V("pc", 144 * i, 144 * i + 144), V("fl", C * i, C * i + 144), V("fl", C * i + 144, C * i + 288), 16.0 * i - 32, A.add, A.add)
        ts(M(3, 5), V("pa", 3, 5), 0.5, A.mult, 200.0, A.add)
        ts(M(0, 3), S("pc", 143, 3, 144), 176.0, A.add)
        ts(M(5, 6), V("pc", 143, 144), 176.0, A.add)
        ts(V("a2"), I(V("at"), M(0, 6)), 2.0, A.mult)
        ts(V("p4", 0, 5), M(0, 5), 4.0, A.mult)
        tt(V("hr"), I(V("at"), M(0, 5)), V("a2", 1, 81), A.add)
        act(V("xh", 0, 704), V("xb", 0, 704), F.Copy, 0.5)
        act(V("xh", 704, 1408), V("xb", 704, 1408), F.Copy, 0.5)
        ts(V("p4", 8, 13), M(0, 5), 175.5, A.is_gt, -1408.0, A.mult)
        tt(V("td"), V("hr"), V("dg"), A.mult)
        ts(V("mm", 0, 80), V("hr"), 2.0 ** 27, A.add, qm, A.is_equal)
        scan(V("te"), V("rz"), V("td"), 0.0, A.mult, A.add)
        hs = S("te", 15, 5, 16)
        ts(V("sm", 24, 29), hs, 2.0 ** 27, A.add, 2.0 ** 27, A.subtract)
        tt(V("sm", 32, 37), hs, V("p4", 0, 5), A.add)
        ts(M(12, 17), hs, 0.0, A.add)
        tt(V("sm", 0, 5), V("sm", 32, 37), V("sm", 24, 29), A.subtract)
        cp(M(6, 11), V("sm", 0, 5))
        tt(V("sm", 16, 21), V("sm", 0, 5), V("p4", 8, 13), A.add)
        send(to, M(0, 18, "lm")[0], M(0, 18)[0], M(0, 18), "al%d" % t)
        act(V("mm", 80, 160), V("mm", 0, 80), F.Copy, 4096.0)
        win = V("vt", 64, 1472)
        cp(I(win, M(6, 11)), V("mm", 0, 80))
        ts(V("o2", 0, 5), V("sm", 16, 21), 704.0, A.add)
        scan(V("lt"), V("kl"), V("zz"), -1000.0, A.add, A.min)
        if t == 0:
            for b in range(4):
                quant("eq", "es", "eb", 128 * b, 128 * b + 128, 4 - b)
        arrive([V(lq), V(ls)], "aq%d" % t, 2 * n_in)
        for b in range(4):
            mx((7, 0, 1, 2)[b], side("eq", "es", b), lq, ls)
        for b in range(4):
            act(V("dx", C * b, C * b + C), P((7, 0, 1, 2)[b]), F.Copy, 0.5)
        tt(V("mm", 160, 240), I(win, V("o2", 0, 5)), V("mm", 80, 160), A.add)
        ts(M(24, 46), S("lt", 15, 22, 16), 15.0, A.add)
        send(to, M(24, 46, "lm")[0], M(24, 46)[0], M(24, 46), "am%d" % t)
        if t == 0:
            iota(V("xr"), [[1, 352]], 0, 0, True)
        cp(I(win, V("o2", 0, 5)), V("mm", 160, 240))
        arrive([M(0, 18, "lm")], "al%d" % t, n_in)
        arrive([M(24, 46, "lm")], "am%d" % t, n_in)
        for u in range(4):
            if u == CVT_AFTER:
                cp(V("cm", 0, 6), M(12, 18, "lm"))
                act(V("cr"), I(V("cm", 0, 8), V("cu", 30, 40)), F.Copy)
            if u:
                act(S("wt", u - 1, 160, 4), S("wt", 1407 + u, 160, 4), F.Copy)
            scan(S("wt", 640 + u, 368, 4), S("vt", 64 + u, 368, 4), S("vt", u, 368, 4), 0.0, A.add, A.subtract)
        act(S("wt", 3, 160, 4), S("wt", 1411, 160, 4), F.Copy)
        tr(V("crt"), V("cr"))
        tt(V("wt", 640, 704), V("wt", 640, 704), V("wt", 2048, 2112), A.add)
        ts(V("pm"), I(V("crt"), V("cu", 40, 45)), 2.0 ** 27, A.add, qm, A.is_equal)
        for j in range(11):
            gl = V("gl", 80 * j, 80 * j + 80)
            tt(gl, I(V("wt", 640 - 64 * j, 2048 - 64 * j), M(6, 11, "lm")), V("pm"), A.mult)
            if j < 9:
                act(V("gj", 80 * j, 80 * j + 80), gl, F.Copy, 1.0, None, V("vx", j, j + 1))
        for j in (9, 10):
            red(V("vx", j, j + 1), V("gl", 80 * j, 80 * j + 80), A.add)
        for b in range(4):
            act(V("db", 96 * b + 16, 96 * b + 96), I(V("dx", C * b, C * b + C), M(0, 5, "lm")), F.Copy)
        act(S("db", 15, 4, 96), S("db", 95, 4, 96), F.Copy)
        if t == ROUNDS - 1:
            act(V("pr", 16, 96), I(V("xr"), M(0, 5, "lm")), F.Copy)
            act(V("pr", 15, 16), V("pr", 95, 96), F.Copy)
        ts(V("vv", 11, 22), V("vx", 0, 11), 2.0 ** 35, A.add, 2.0 ** 35, A.subtract)
        tt(V("vv", 0, 11), V("vx", 0, 11), V("vv", 11, 22), A.subtract)
        cp(V("cm", 8, 30), M(24, 46, "lm"))
        tr(V("vvt"), V("vv"))
        cp(V("cm", 30, 52), M(24, 46, "lm"))
        scan(V("sab"), V("rz", 0, 32), V("vvt"), 0.0, A.mult, A.add)
        ts(V("s2"), I(V("sab"), V("cu", 48, 50)), V("cf", 2, 3), A.mult, V("cf", 3, 4), A.add)
        if t == 0:
            quant("vq", "vs", "vb", 0, 128)
        tr(V("s2t"), V("s2"))
        red(V("bs", 0, 1), V("s2t"), A.max)
        ts(V("bs", 1, 2), V("bs", 0, 1), 2.0 ** 29, A.add, 2.0 ** 29, A.subtract)
        ts(V("ro"), V("cf", 14, 16), V("bs", 1, 2), A.add, V("bs", 0, 1), A.subtract)
        cp(V("fo"), I(V("cm"), V("ro")))
        nq, ns = "qx%d" % (t + 1), "sx%d" % (t + 1)
        nxt = side("uq", "us", 0) if t < ROUNDS - 1 else side("vq", "vs", 0)

        def zpart(b, a, e):
            tt(S("zt", 4 * a + b, e - a, 4), I(V("db", 96 * b, 96 * b + 96), V("fo", a // 16, e // 16)), S("xh", 4 * a + b, e - a, 4), A.add)

        def layer(h):
            quant("zq", "zs", "zt", *pieces[h])
            for b in range(4):
                mx(4 * h + b, side("wq", "wsc", b), "zq", "zs", *pieces[h])

        def state(h, b):
            a, e = pieces[h]
            x32 = S("x32", 4 * a + b, e - a, 4)
            tt(x32, P(4 * h + b, e - a), x32, A.add)
            if (h, b) == (1, 3):
                quant(nq, ns, "xb", 0, H)
                mx(0, nxt, nq, ns, 0, H)
                ts(S("xb", 4 * a + b, e - a, 4), x32, 0.03125, A.mult)
            else:
                act(S("xb", 4 * a + b, e - a, 4), x32, F.Copy, 0.03125)
        if t == 0:
            act(V("x32"), V("xb"), F.Copy, 32.0)
        zpart(0, 0, C)
        if t == ROUNDS - 1:
            act(V("olr"), I(V("pr"), V("fo", 0, 22)), F.Copy)
            store("s", T.ol[:, :], T.olr[0:128:16, :], V("olr"))
        for b in (1, 2, 3):
            zpart(b, 0, H)
        zpart(1, H, C)
        layer(0)
        zpart(2, H, C)
        zpart(3, H, C)
        state(0, 0)
        layer(1)
        for k in range(1, 8):
            state(k // 4, k % 4)
        quant(nq, ns, "xb", H, C)
        mx(1, nxt, nq, ns, H, C)
    act(V("yb", 0, H), P(0, H), F.Copy)
    store("a", T.y[:, 0:H], T.yb[:, 0:H], V("yb", 0, H))
    store("s", T.oc[:, :], U8(V("qx3")), V("qx3"))
    cp(V("yb", H, C), P(1, C - H))
    store("s", T.y[:, H:C], T.yb[:, H:C], V("yb", H, C))
    for k in range(4):
        store("a", T.osc[4 * k:4 * k + 4, :], T.sx3[32 * k:32 * k + 4, :], V("sx3"))

    emit(T, eng, ops)
    g.sync.wait_ge(T.sem.stored, totals["stored"])
    g.wait_ge(T.sem.sent, totals["sent"])


def emit(T, eng, ops):
    hist, known, clocks, waits, marked = {}, {q: {} for q in eng}, [], [], set()
    for i, o in enumerate(ops):
        q, deps, need = o["q"], set(), []
        for name, bits in o["rd"]:
            deps.update(j for j, w, b in hist.get(name, ()) if b & bits and (w or (name == "ps" and ops[j]["q"] != q)))
        for name, bits in o["wr"]:
            deps.update(j for j, w, b in hist.get(name, ()) if b & bits)
        for name, bits in o["wr"]:
            hist[name] = [(j, w, b & ~bits) for j, w, b in hist.get(name, ()) if b & ~bits] + [(i, True, bits)]
        for name, bits in o["rd"]:
            hist.setdefault(name, []).append((i, False, bits))
        kn = known.get(q, {})
        for j in sorted(deps, reverse=True):
            key = ops[j]["sem"] or ops[j]["q"]
            if q is None or kn.get(key, -1) >= j:
                continue
            need.append(j)
            marked.add(j)
            kn[key] = j
            for k2, v2 in clocks[j].items():
                kn[k2] = max(kn.get(k2, -1), v2)
        clocks.append(dict(kn))
        waits.append(need)
    count, value = {q: 0 for q in eng}, {}
    for i, o in enumerate(ops):
        q = o["q"]
        value[i] = (o["sem"], o["count"])
        if q is None:
            continue
        for j in waits[i]:
            eng[q].wait_ge(T.sem[value[j][0]], value[j][1])
        ins = o["fn"]()
        if o["sem"]:
            ins.then_inc(T.sem[o["sem"]], o["count"])
        elif i in marked:
            count[q] += 1
            ins.then_inc(T.sem["q" + q], 1)
            value[i] = ("q" + q, count[q])
